import numpy as np
import ml_dtypes


def mxq(x, axis, fmt="e4m3"):
    dtype, down = {"e4m3": (ml_dtypes.float8_e4m3fn, 7), "e5m2": (ml_dtypes.float8_e5m2, 14)}[fmt]
    v = np.moveaxis(np.asarray(x, np.float32).astype(ml_dtypes.bfloat16).astype(np.float64), axis, -1)
    blocks = v.reshape(v.shape[:-1] + (-1, 32))
    amax = np.abs(blocks).max(-1, keepdims=True)
    byte = np.maximum(np.where(amax > 0, np.frexp(amax)[1] - 1 + 127, 0) - down, 1)
    scale = np.exp2(byte - 127.0)
    codes = (blocks / scale).astype(np.float32).astype(dtype).astype(np.float64)
    return np.moveaxis((codes * scale).reshape(v.shape), -1, axis)


WIDE = False


def mx_kscale(k):
    if not WIDE:
        return np.ones(k)
    levels = np.array([10, -10, 5, -5, 0])
    if k % 512:
        return np.exp2(np.random.permutation(np.resize(levels, k // 32))).repeat(32)
    a = np.empty((k // 512, 16))
    for p in range(k // 512):
        a[p, :8] = np.random.permutation(np.resize(levels, 8))
        for g in range(8):
            far = levels[np.abs(levels - a[p, g]) >= 10]
            a[p, g + 8] = far[np.random.randint(len(far))]
    return np.exp2(a.ravel()).repeat(32)


def f64(x):
    return np.asarray(x).astype(np.float64)


def striped(idx):
    return np.tile(idx.reshape(-1, 16).T, (8, 1)).astype(np.uint16)


def unstriped(offs):
    return offs[:16].T.reshape(-1).astype(np.int64)


E2M1 = np.array([0.0, 0.5, 1.0, 1.5, 2.0, 3.0, 4.0, 6.0, -0.0, -0.5, -1.0, -1.5, -2.0, -3.0, -4.0, -6.0])


def pack_weight(w, fmt):
    k, n = w.shape
    w = f64(np.asarray(w, np.float32).astype(ml_dtypes.bfloat16)).reshape(k // 32, 32, n)
    amax = np.abs(w).max(1)
    if fmt == "e4m3":
        byte = np.frexp(amax)[1] - 1 + 127 - 7
    else:
        mant, ex = np.frexp(amax / 6.0)
        byte = np.where(mant > 0.5, ex, ex - 1) + 127
    byte = np.clip(np.where(amax > 0, byte, 1), 1, 254)
    scaled = (w * np.exp2(127.0 - byte)[:, None, :]).reshape(k, n).astype(np.float32)
    by_word = np.ascontiguousarray(scaled.reshape(k // 512, 128, 4, n).transpose(0, 1, 3, 2))
    if fmt == "e4m3":
        words = by_word.astype(ml_dtypes.float8_e4m3fn).view(np.uint8)
    else:
        c = by_word.astype(ml_dtypes.float4_e2m1fn).view(np.uint8) & 0xF
        words = (c[..., 0::2] | (c[..., 1::2] << 4)).reshape(k // 512, 128, 2 * n)
    return np.ascontiguousarray(words), np.ascontiguousarray(byte.astype(np.uint8).reshape(k // 512, 16, n))


def unpack_weight(words, scales, fmt):
    g, _, n = scales.shape
    words = np.ascontiguousarray(words).reshape(g, 128, n, -1)
    if fmt == "e4m3":
        vals = words.view(ml_dtypes.float8_e4m3fn).astype(np.float64)
    else:
        nib = np.empty((g, 128, n, 4), np.uint8)
        nib[..., 0::2] = words & 0xF
        nib[..., 1::2] = words >> 4
        vals = E2M1[nib]
    vals = vals * np.repeat(np.exp2(scales.astype(np.float64) - 127.0), 8, axis=1)[..., None]
    return vals.transpose(0, 1, 3, 2).reshape(g * 512, n)


def silu(v):
    return v / (1.0 + np.exp(-np.maximum(v, -700.0)))


def d_silu(v):
    s = 1.0 / (1.0 + np.exp(-np.maximum(v, -700.0)))
    return s * (1.0 + v * (1.0 - s))


K, T, E, C, H, N = 768, 512, 4, 256, 512, 1024


def by_expert(wq, xq):
    return np.concatenate([wq[e].T @ xq[:, e * C:(e + 1) * C] for e in range(E)], axis=1)


def setup_inputs():
    n = np.random.standard_normal
    s = mx_kscale(N)[:, None]
    u = mx_kscale(H)
    first = np.random.permutation(np.repeat(np.arange(E), T // E))
    second = (first + 1 + np.random.permutation(np.repeat(np.arange(E - 1), -(-T // (E - 1)))[:T])) % E
    while np.bincount(second, minlength=E).max() != T // E:
        load = np.bincount(second, minlength=E); hi, lo = int(load.argmax()), int(load.argmin())
        t = np.flatnonzero((second == hi) & (first != lo))[0]; second[t] = lo
    slot_token = np.empty(E * C, np.int64); pos = np.empty((2, T), np.int64); fill = np.zeros(E, np.int64)
    place = np.stack([np.random.permutation(C) for _ in range(E)])
    for r, deal in enumerate((first, second)):
        for t in np.random.permutation(T):
            e = deal[t]; j = e * C + place[e, fill[e]]; fill[e] += 1; slot_token[j] = t; pos[r, t] = j
    g = np.random.uniform(0.2, 0.8, T)
    w_slot = np.empty(E * C); w_slot[pos[0]] = g; w_slot[pos[1]] = 1.0 - g
    w2 = [pack_weight(m, "e2m1") for m in n((E, N, H)) / np.sqrt(N) / s[None] * u[None, None, :]]
    w1 = [pack_weight(m, "e2m1") for m in n((E, H, K)) / np.sqrt(H) / u[None, :, None]]
    w3 = [pack_weight(m, "e2m1") for m in n((E, H, K)) / np.sqrt(H) / u[None, :, None]]
    return {
        "dyT": (n((N, T)) * s).astype(np.float32),
        "a1": n((H, E * C)).astype(np.float32),
        "a3": n((H, E * C)).astype(np.float32),
        "w2_words": np.stack([m[0] for m in w2]),
        "w2_scales": np.stack([m[1] for m in w2]),
        "w1_words": np.stack([m[0] for m in w1]),
        "w1_scales": np.stack([m[1] for m in w1]),
        "w3_words": np.stack([m[0] for m in w3]),
        "w3_scales": np.stack([m[1] for m in w3]),
        "gate": np.tile(w_slot, (N, 1)).astype(np.float32),
        "offs": striped(slot_token),
        "pos1": striped(pos[0]),
        "pos2": striped(pos[1]),
    }


def reference(dyT, a1, a3, w2_words, w2_scales, w1_words, w1_scales, w3_words, w3_scales, gate, offs, pos1, pos2):
    idx = unstriped(offs)
    w2 = np.stack([unpack_weight(w2_words[e], w2_scales[e], "e2m1") for e in range(E)])
    w1 = np.stack([unpack_weight(w1_words[e], w1_scales[e], "e2m1") for e in range(E)])
    w3 = np.stack([unpack_weight(w3_words[e], w3_scales[e], "e2m1") for e in range(E)])
    gq = mxq(f64(gate) * f64(dyT)[:, idx], 0, "e4m3")
    dh = by_expert(w2, gq)
    da1 = dh * f64(a3) * d_silu(f64(a1))
    da3 = dh * silu(f64(a1))
    dx = by_expert(w1, mxq(da1, 0, "e4m3")) + by_expert(w3, mxq(da3, 0, "e4m3"))
    return dx[:, unstriped(pos1)] + dx[:, unstriped(pos2)]

@@ -1,0 +1,259 @@
+from contextlib import ExitStack
+
+import concourse.mybir as mybir
+from concourse.masks import make_identity
+
+K, T, E, C, H, N = 768, 512, 4, 256, 512, 1024
+S = E * C
+
+FLOPS = 2 * S * (N * H + 2 * H * K)
+BYTES = 4 * (N * T + 2 * H * S + S + K * T) + E * (N * H // 2 + N * H // 32) + 2 * E * (H * K // 2 + H * K // 32) + 2 * (S + 2 * T) * 8
+
+F32 = mybir.dt.float32
+BF16 = mybir.dt.bfloat16
+U32 = mybir.dt.uint32
+I32 = mybir.dt.int32
+U16 = mybir.dt.uint16
+U8 = mybir.dt.uint8
+E4M3X4 = mybir.dt.float8_e4m3fn_x4
+E2M1X4 = mybir.dt.float4_e2m1fn_x4
+ACT = mybir.ActivationFunctionType
+MULT = mybir.AluOpType.mult
+SUB = mybir.AluOpType.subtract
+ADD = mybir.AluOpType.add
+
+P = 128
+HALF = 128
+NPASS = N // 512
+KT = K // P
+
+
+def tile_moe_bdx_glu_silu_kernel(
+    tc, dyT, a1, a3, w2_words, w2_scales, w1_words, w1_scales, w3_words, w3_scales, gate, offs, pos1, pos2, out
+):
+    nc = tc.nc
+    with ExitStack() as ctx:
+        keep = ctx.enter_context(tc.tile_pool(name="keep", bufs=1))
+        ring3 = ctx.enter_context(tc.tile_pool(name="ring3", bufs=3))
+        ring2 = ctx.enter_context(tc.tile_pool(name="ring2", bufs=2))
+        psum = ctx.enter_context(tc.psum_pool(name="psum", bufs=2))
+
+        offs_t = keep.tile([P, S // 16], U16, name="offs_t")
+        pos1_t = keep.tile([P, T // 16], U16, name="pos1_t")
+        pos2_t = keep.tile([P, T // 16], U16, name="pos2_t")
+        dy = [[keep.tile([P, T], F32, name=f"dy{s}{t}") for t in range(4)] for s in range(NPASS)]
+        gate_t = keep.tile([P, S], F32, name="gate_t")
+        a1_t = keep.tile([P, 4, S], F32, name="a1_t")
+        a3_t = keep.tile([P, 4, S], F32, name="a3_t")
+        w2_t = keep.tile([P, E * NPASS, 2 * H], U8, name="w2_t", align_bytes=64)
+        w2s_t = keep.tile([P, E * NPASS, H], U8, name="w2s_t", align_bytes=64)
+        w13_t = [keep.tile([P, E, 2 * K], U8, name=f"w13_t{j}", align_bytes=64) for j in range(2)]
+        w13s_t = [keep.tile([P, E, K], U8, name=f"w13s_t{j}", align_bytes=64) for j in range(2)]
+        ident = keep.tile([P, P], F32, name="ident")
+        dx_t = keep.tile([P, KT, S], F32, name="dx_t")
+
+        nc.gpsimd.memset(w2s_t[:].bitcast(I32), 0)
+        nc.gpsimd.memset(w13s_t[0][:].bitcast(I32), 0)
+        nc.gpsimd.memset(w13s_t[1][:].bitcast(I32), 0)
+        make_identity(nc, ident[:])
+
+        def load_dy(s, t):
+            rows = dyT[512 * s : 512 * (s + 1), :].rearrange("(p t) n -> t p n", t=4)
+            nc.sync.dma_start(out=dy[s][t][:], in_=rows[t])
+
+        def load_w2(e):
+            src = w2_words.bitcast(I32).rearrange("e s p n -> p (e s) n")
+            es = slice(e * NPASS, (e + 1) * NPASS)
+            nc.sync.dma_start(out=w2_t[:, es, :].bitcast(I32), in_=src[:, es, :])
+
+        def load_scales(dst, src):
+            view = src.bitcast(I32).rearrange("e s (q r) i -> r q (e s) i", r=4)
+            for r in range(4):
+                nc.sync.dma_start(out=dst[:].bitcast(I32)[r : P : 32, :, :], in_=view[r])
+
+        def load_a(dst, src, e):
+            cols = slice(e * C, (e + 1) * C)
+            nc.sync.dma_start(out=dst[:, :, cols], in_=src.rearrange("(p t) n -> p t n", t=4)[:, :, cols])
+
+        nc.sync.dma_start(offs_t[:], offs)
+        load_dy(0, 0)
+        nc.sync.dma_start(out=gate_t[:, 0:C], in_=gate[0:P, 0:C])
+        for i in range(1, 8):
+            load_dy(i // 4, i % 4)
+        load_w2(0)
+        nc.sync.dma_start(out=gate_t[:, C:S], in_=gate[0:P, C:S])
+        load_scales(w2s_t, w2_scales)
+        for e in range(E):
+            load_a(a1_t, a1, e)
+        load_w2(1)
+        load_a(a3_t, a3, 0)
+        load_w2(2)
+        load_w2(3)
+        for j, (words, scales) in enumerate(((w1_words, w1_scales), (w3_words, w3_scales))):
+            nc.sync.dma_start(out=w13_t[j][:].bitcast(I32), in_=words.bitcast(I32).rearrange("e s p n -> p (e s) n"))
+            load_scales(w13s_t[j], scales)
+        for e in range(1, E):
+            load_a(a3_t, a3, e)
+        nc.sync.dma_start(pos1_t[:], pos1)
+        nc.sync.dma_start(pos2_t[:], pos2)
+
+        codes = [keep.tile([P, NPASS, C], U32, name=f"codes{e}", align_bytes=64) for e in range(E)]
+        scales_g = [keep.tile([P, NPASS, C], U8, name=f"scales_g{e}", align_bytes=64) for e in range(E)]
+        grouped = {}
+
+        def gather(e, s):
+            g4 = ring3.tile([P, 4, C], F32, name="g4")
+            for t in range(4):
+                nc.vector.tensor_tensor(
+                    g4[:, t, :], dy[s][t][:].indirect(offs_t[:, e * C // 16 : (e + 1) * C // 16]), gate_t[:, e * C : (e + 1) * C], MULT
+                )
+            gb = ring3.tile([P, C, 4], BF16, name="gb", align_bytes=64)
+            nc.scalar.copy(
+                out=gb[:].rearrange("p (c i) t -> p c t i", i=4), in_=g4[:].rearrange("p t (c i) -> p c t i", i=4)
+            )
+            grouped[e, s] = gb
+
+        def quantize_g(e, s):
+            nc.vector.quantize_mx(
+                out=codes[e][:, s, :].bitcast(E4M3X4), scales=scales_g[e][:, s, :], in_=grouped[e, s][:].rearrange("p n t -> p (n t)")
+            )
+
+        dh = {}
+
+        def first_product(e, h):
+            cols = slice(h * HALF, (h + 1) * HALF)
+            dht = psum.tile([P, H], F32, name="dht")
+            for s in range(NPASS):
+                nc.tensor.matmul_mx(
+                    out=dht[:],
+                    lhsT=codes[e][:, s, cols].bitcast(E4M3X4),
+                    lhsT_scale=scales_g[e][:, s, cols],
+                    rhs=w2_t[:, e * NPASS + s, :].bitcast(E2M1X4),
+                    rhs_scale=w2s_t[:, e * NPASS + s, :],
+                    start=(s == 0),
+                    stop=(s == NPASS - 1),
+                )
+            turned = ring3.tile([P, 4, P], F32, name="turned")
+            nc.scalar.copy(out=turned[:], in_=dht[:].rearrange("p (q t) -> p t q", t=4))
+            bank = psum.tile([P, 4, HALF], F32, name="bank")
+            for t in range(4):
+                nc.tensor.transpose(bank[:, t, :], turned[:, t, :], ident[:])
+            dh[e, h] = bank
+
+        silu_t = keep.tile([P, 4, S], F32, name="silu_t")
+        nsilu_t = keep.tile([P, 4, S], F32, name="nsilu_t")
+        sig_t = keep.tile([P, 4, S], F32, name="sig_t")
+        f1_t = keep.tile([P, 4, S], F32, name="f1_t")
+
+        def silus(e):
+            cols = slice(e * C, (e + 1) * C)
+            nc.scalar.activation(nsilu_t[:, :, cols], a1_t[:, :, cols], ACT.Silu, scale=-1.0)
+            nc.scalar.activation(silu_t[:, :, cols], a1_t[:, :, cols], ACT.Silu)
+
+        def sigmoids(cols):
+            nc.scalar.activation(sig_t[:, :, cols], a1_t[:, :, cols], ACT.Sigmoid)
+
+        def factor(e):
+            cols = slice(e * C, (e + 1) * C)
+            nd = ring2.tile([P, 4, C], F32, name="nd")
+            nc.vector.scalar_tensor_tensor(nd[:], nsilu_t[:, :, cols], 1.0, sig_t[:, :, cols], SUB, MULT)
+            nc.vector.scalar_tensor_tensor(f1_t[:, :, cols], nd[:], -1.0, a3_t[:, :, cols], MULT, MULT)
+
+        qd = {}
+
+        def products(e, h):
+            da = ring3.tile([P, 2, HALF, 4], BF16, name="da", align_bytes=64)
+            cols = slice(e * C + h * HALF, e * C + (h + 1) * HALF)
+            for j, f in enumerate((f1_t, silu_t)):
+                nc.vector.tensor_tensor(
+                    da[:, j].rearrange("p (c i) t -> p c t i", i=4),
+                    dh[e, h][:].rearrange("p t (c i) -> p c t i", i=4),
+                    f[:, :, cols].rearrange("p t (c i) -> p c t i", i=4),
+                    MULT,
+                )
+            qd[e, h] = da
+
+        def second(e, h):
+            dc = ring3.tile([P, 2, HALF], U32, name="dc", align_bytes=64)
+            ds = ring3.tile([P, 2, HALF], U8, name="ds", align_bytes=64)
+            nc.vector.quantize_mx(
+                out=dc[:].rearrange("p j n -> p (j n)").bitcast(E4M3X4),
+                scales=ds[:].rearrange("p j n -> p (j n)"),
+                in_=qd[e, h][:].rearrange("p j n t -> p (j n t)"),
+            )
+            for k0 in (0, 3):
+                acc = psum.tile([P, 3, HALF], F32, name=f"acc{k0}")
+                for k in range(3):
+                    kt = k0 + k
+                    for j in range(2):
+                        nc.tensor.matmul_mx(
+                            out=acc[:, k, :],
+                            lhsT=w13_t[j][:, e, 2 * P * kt : 2 * P * (kt + 1)].bitcast(E2M1X4),
+                            lhsT_scale=w13s_t[j][:, e, P * kt : P * (kt + 1)],
+                            rhs=dc[:, j, :].bitcast(E4M3X4),
+                            rhs_scale=ds[:, j, :],
+                            start=(j == 0),
+                            stop=(j == 1),
+                        )
+                nc.scalar.copy(out=dx_t[:, k0 : k0 + 3, e * C + h * HALF : e * C + (h + 1) * HALF], in_=acc[:])
+
+        def combine(kt):
+            r1 = ring2.tile([P, T], F32, name="r1")
+            nc.vector.tensor_copy(r1[:], dx_t[:, kt, :].indirect(pos1_t[:]))
+            r2 = ring2.tile([P, T], F32, name="r2")
+            nc.vector.tensor_copy(r2[:], dx_t[:, kt, :].indirect(pos2_t[:]))
+            o = ring2.tile([P, T], F32, name="o")
+            eng = nc.vector if kt == KT - 1 else nc.gpsimd
+            eng.tensor_tensor(o[:], r1[:], r2[:], ADD)
+            nc.sync.dma_start(out=out[kt * P : (kt + 1) * P, :], in_=o[:])
+
+        gather(0, 0)
+        gather(0, 1)
+        quantize_g(0, 0)
+        gather(1, 0)
+        quantize_g(0, 1)
+        first_product(0, 0)
+        first_product(0, 1)
+        gather(1, 1)
+        for e in range(E):
+            silus(e)
+        quantize_g(1, 0)
+        gather(2, 0)
+        quantize_g(1, 1)
+        first_product(1, 0)
+        gather(2, 1)
+        sigmoids(slice(0, S // 2))
+        quantize_g(2, 0)
+        factor(0)
+        quantize_g(2, 1)
+        products(0, 0)
+        products(0, 1)
+        second(0, 0)
+        first_product(1, 1)
+        second(0, 1)
+        gather(3, 0)
+        sigmoids(slice(S // 2, S))
+        gather(3, 1)
+        quantize_g(3, 0)
+        factor(1)
+        quantize_g(3, 1)
+        products(1, 0)
+        first_product(2, 0)
+        products(1, 1)
+        second(1, 0)
+        first_product(2, 1)
+        second(1, 1)
+        factor(2)
+        products(2, 0)
+        first_product(3, 0)
+        products(2, 1)
+        second(2, 0)
+        first_product(3, 1)
+        second(2, 1)
+        factor(3)
+        products(3, 0)
+        products(3, 1)
+        second(3, 0)
+        second(3, 1)
+        for kt in range(KT):
+            combine(kt)

@@ -75,25 +75,36 @@ def tile_moe_bdx_glu_silu_kernel(
             cols = slice(e * C, (e + 1) * C)
             nc.sync.dma_start(out=dst[:, :, cols], in_=src.rearrange("(p t) n -> p t n", t=4)[:, :, cols])
 
+        def load_gate(e):
+            nc.sync.dma_start(out=gate_t[:, e * C : (e + 1) * C], in_=gate[0:P, e * C : (e + 1) * C])
+
         nc.sync.dma_start(offs_t[:], offs)
+        load_gate(0)
         load_dy(0, 0)
-        nc.sync.dma_start(out=gate_t[:, 0:C], in_=gate[0:P, 0:C])
-        for i in range(1, 8):
-            load_dy(i // 4, i % 4)
+        load_dy(0, 1)
+        load_dy(0, 2)
+        load_gate(1)
+        load_dy(0, 3)
+        load_a(a1_t, a1, 0)
+        for t in range(4):
+            load_dy(1, t)
+        load_a(a1_t, a1, 1)
         load_w2(0)
-        nc.sync.dma_start(out=gate_t[:, C:S], in_=gate[0:P, C:S])
         load_scales(w2s_t, w2_scales)
-        for e in range(E):
-            load_a(a1_t, a1, e)
+        load_gate(2)
+        load_gate(3)
         load_w2(1)
         load_a(a3_t, a3, 0)
+        load_a(a1_t, a1, 2)
+        load_a(a1_t, a1, 3)
         load_w2(2)
         load_w2(3)
+        load_a(a3_t, a3, 1)
         for j, (words, scales) in enumerate(((w1_words, w1_scales), (w3_words, w3_scales))):
             nc.sync.dma_start(out=w13_t[j][:].bitcast(I32), in_=words.bitcast(I32).rearrange("e s p n -> p (e s) n"))
             load_scales(w13s_t[j], scales)
-        for e in range(1, E):
-            load_a(a3_t, a3, e)
+        load_a(a3_t, a3, 2)
+        load_a(a3_t, a3, 3)
         nc.sync.dma_start(pos1_t[:], pos1)
         nc.sync.dma_start(pos2_t[:], pos2)
 
@@ -181,9 +192,10 @@ def tile_moe_bdx_glu_silu_kernel(
                 scales=ds[:].rearrange("p j n -> p (j n)"),
                 in_=qd[e, h][:].rearrange("p j n t -> p (j n t)"),
             )
-            for k0 in (0, 3):
-                acc = psum.tile([P, 3, HALF], F32, name=f"acc{k0}")
-                for k in range(3):
+            groups = ((0, 1), (1, 2), (3, 3)) if (e, h) == (E - 1, 1) else ((0, 3), (3, 3))
+            for i, (k0, kn) in enumerate(groups):
+                acc = psum.tile([P, kn, HALF], F32, name=f"acc{i % 2}")
+                for k in range(kn):
                     kt = k0 + k
                     for j in range(2):
                         nc.tensor.matmul_mx(
@@ -195,65 +207,54 @@ def tile_moe_bdx_glu_silu_kernel(
                             start=(j == 0),
                             stop=(j == 1),
                         )
-                nc.scalar.copy(out=dx_t[:, k0 : k0 + 3, e * C + h * HALF : e * C + (h + 1) * HALF], in_=acc[:])
+                nc.scalar.copy(out=dx_t[:, k0 : k0 + kn, e * C + h * HALF : e * C + (h + 1) * HALF], in_=acc[:])
 
-        def combine(kt):
-            r1 = ring2.tile([P, T], F32, name="r1")
-            nc.vector.tensor_copy(r1[:], dx_t[:, kt, :].indirect(pos1_t[:]))
-            r2 = ring2.tile([P, T], F32, name="r2")
-            nc.vector.tensor_copy(r2[:], dx_t[:, kt, :].indirect(pos2_t[:]))
-            o = ring2.tile([P, T], F32, name="o")
-            eng = nc.vector if kt == KT - 1 else nc.gpsimd
+        def combine(kt, c0, cn, eng):
+            cols = slice(c0 // 16, (c0 + cn) // 16)
+            r1 = ring2.tile([P, cn], F32, name="r1")
+            nc.vector.tensor_copy(r1[:], dx_t[:, kt, :].indirect(pos1_t[:, cols]))
+            r2 = ring2.tile([P, cn], F32, name="r2")
+            nc.vector.tensor_copy(r2[:], dx_t[:, kt, :].indirect(pos2_t[:, cols]))
+            o = ring2.tile([P, cn], F32, name="o")
             eng.tensor_tensor(o[:], r1[:], r2[:], ADD)
-            nc.sync.dma_start(out=out[kt * P : (kt + 1) * P, :], in_=o[:])
+            nc.sync.dma_start(out=out[kt * P : (kt + 1) * P, c0 : c0 + cn], in_=o[:])
 
         gather(0, 0)
-        gather(0, 1)
-        quantize_g(0, 0)
         gather(1, 0)
+        quantize_g(0, 0)
+        gather(0, 1)
+        quantize_g(1, 0)
+        silus(0)
+        gather(1, 1)
         quantize_g(0, 1)
         first_product(0, 0)
-        first_product(0, 1)
-        gather(1, 1)
-        for e in range(E):
-            silus(e)
-        quantize_g(1, 0)
+        silus(1)
         gather(2, 0)
         quantize_g(1, 1)
-        first_product(1, 0)
+        first_product(0, 1)
+        sigmoids(slice(0, 2 * C))
         gather(2, 1)
-        sigmoids(slice(0, S // 2))
         quantize_g(2, 0)
-        factor(0)
-        quantize_g(2, 1)
-        products(0, 0)
-        products(0, 1)
-        second(0, 0)
-        first_product(1, 1)
-        second(0, 1)
         gather(3, 0)
-        sigmoids(slice(S // 2, S))
+        quantize_g(2, 1)
+        silus(2)
+        silus(3)
         gather(3, 1)
         quantize_g(3, 0)
-        factor(1)
-        quantize_g(3, 1)
-        products(1, 0)
-        first_product(2, 0)
-        products(1, 1)
-        second(1, 0)
-        first_product(2, 1)
-        second(1, 1)
-        factor(2)
-        products(2, 0)
-        first_product(3, 0)
-        products(2, 1)
-        second(2, 0)
-        first_product(3, 1)
-        second(2, 1)
-        factor(3)
-        products(3, 0)
-        products(3, 1)
-        second(3, 0)
-        second(3, 1)
-        for kt in range(KT):
-            combine(kt)
+        sigmoids(slice(2 * C, 4 * C))
+        for e in range(E):
+            factor(e)
+            if e == 0:
+                quantize_g(3, 1)
+            products(e, 0)
+            if e + 1 < E:
+                first_product(e + 1, 0)
+            products(e, 1)
+            second(e, 0)
+            if e + 1 < E:
+                first_product(e + 1, 1)
+            second(e, 1)
+        for kt in range(KT - 1):
+            combine(kt, 0, T, nc.gpsimd)
+        combine(KT - 1, 0, T // 2, nc.vector)
+        combine(KT - 1, T // 2, T // 2, nc.vector)

@@ -26,6 +26,7 @@ P = 128
 HALF = 128
 NPASS = N // 512
 KT = K // P
+CUTS = ((0, 256), (256, 384), (640, 384))
 
 
 def tile_moe_bdx_glu_silu_kernel(
@@ -43,14 +44,14 @@ def tile_moe_bdx_glu_silu_kernel(
         pos2_t = keep.tile([P, T // 16], U16, name="pos2_t")
         dy = [[keep.tile([P, T], F32, name=f"dy{s}{t}") for t in range(4)] for s in range(NPASS)]
         gate_t = keep.tile([P, S], F32, name="gate_t")
-        a1_t = keep.tile([P, 4, S], F32, name="a1_t")
-        a3_t = keep.tile([P, 4, S], F32, name="a3_t")
+        a1_t = [keep.tile([P, 4, 2 * C], F32, name=f"a1_t{i}") for i in range(2)]
+        a3_t = [keep.tile([P, 4, C], F32, name=f"a3_t{e}") for e in range(E)]
         w2_t = keep.tile([P, E * NPASS, 2 * H], U8, name="w2_t", align_bytes=64)
         w2s_t = keep.tile([P, E * NPASS, H], U8, name="w2s_t", align_bytes=64)
         w13_t = [keep.tile([P, E, 2 * K], U8, name=f"w13_t{j}", align_bytes=64) for j in range(2)]
         w13s_t = [keep.tile([P, E, K], U8, name=f"w13s_t{j}", align_bytes=64) for j in range(2)]
         ident = keep.tile([P, P], F32, name="ident")
-        dx_t = keep.tile([P, KT, S], F32, name="dx_t")
+        dummy = keep.tile([P, 1], F32, name="dummy")
 
         nc.gpsimd.memset(w2s_t[:].bitcast(I32), 0)
         nc.gpsimd.memset(w13s_t[0][:].bitcast(I32), 0)
@@ -73,30 +74,34 @@ def tile_moe_bdx_glu_silu_kernel(
 
         def load_a(dst, src, e):
             cols = slice(e * C, (e + 1) * C)
-            nc.sync.dma_start(out=dst[:, :, cols], in_=src.rearrange("(p t) n -> p t n", t=4)[:, :, cols])
+            nc.sync.dma_start(out=dst[e][:], in_=src.rearrange("(p t) n -> p t n", t=4)[:, :, cols])
+
+        def load_a1(i):
+            cols = slice(2 * i * C, 2 * (i + 1) * C)
+            nc.sync.dma_start(out=a1_t[i][:], in_=a1.rearrange("(p t) n -> p t n", t=4)[:, :, cols])
 
         def load_gate(e):
             nc.sync.dma_start(out=gate_t[:, e * C : (e + 1) * C], in_=gate[0:P, e * C : (e + 1) * C])
 
+        nc.vector.memset(dummy[:], 0.0)
+        nc.scalar.activation(dummy[:], dummy[:], ACT.Silu)
+
+        nc.scalar.dma_start(out=gate_t[:, 0:C], in_=gate[0:P, 0:C])
         nc.sync.dma_start(offs_t[:], offs)
-        load_gate(0)
         load_dy(0, 0)
+        for e in range(1, E):
+            load_gate(e)
         load_dy(0, 1)
+        load_a1(0)
         load_dy(0, 2)
-        load_gate(1)
         load_dy(0, 3)
-        load_a(a1_t, a1, 0)
+        load_a1(1)
         for t in range(4):
             load_dy(1, t)
-        load_a(a1_t, a1, 1)
         load_w2(0)
         load_scales(w2s_t, w2_scales)
-        load_gate(2)
-        load_gate(3)
         load_w2(1)
         load_a(a3_t, a3, 0)
-        load_a(a1_t, a1, 2)
-        load_a(a1_t, a1, 3)
         load_w2(2)
         load_w2(3)
         load_a(a3_t, a3, 1)
@@ -108,80 +113,98 @@ def tile_moe_bdx_glu_silu_kernel(
         nc.sync.dma_start(pos1_t[:], pos1)
         nc.sync.dma_start(pos2_t[:], pos2)
 
-        codes = [keep.tile([P, NPASS, C], U32, name=f"codes{e}", align_bytes=64) for e in range(E)]
-        scales_g = [keep.tile([P, NPASS, C], U8, name=f"scales_g{e}", align_bytes=64) for e in range(E)]
-        grouped = {}
+        codes = keep.tile([P, NPASS, S], U32, name="codes", align_bytes=64)
+        scales_g = keep.tile([P, NPASS, S], U8, name="scales_g", align_bytes=64)
+        grouped = [keep.tile([P, S, 4], BF16, name=f"grouped{s}", align_bytes=64) for s in range(NPASS)]
 
-        def gather(e, s):
-            g4 = ring3.tile([P, 4, C], F32, name="g4")
-            for t in range(4):
-                nc.vector.tensor_tensor(
-                    g4[:, t, :], dy[s][t][:].indirect(offs_t[:, e * C // 16 : (e + 1) * C // 16]), gate_t[:, e * C : (e + 1) * C], MULT
-                )
-            gb = ring3.tile([P, C, 4], BF16, name="gb", align_bytes=64)
-            nc.scalar.copy(
-                out=gb[:].rearrange("p (c i) t -> p c t i", i=4), in_=g4[:].rearrange("p t (c i) -> p c t i", i=4)
+        g_first = [keep.tile([P, 4, cn], F32, name=f"g_first{c0}") for c0, cn in CUTS]
+
+        def look_up(dst, s, t, c0, cn):
+            nc.vector.tensor_tensor(
+                dst, dy[s][t][:].indirect(offs_t[:, c0 // 16 : (c0 + cn) // 16]), gate_t[:, c0 : c0 + cn], MULT
             )
-            grouped[e, s] = gb
 
-        def quantize_g(e, s):
+        def interleave(s, src, c0, cn):
+            nc.scalar.copy(
+                out=grouped[s][:, c0 : c0 + cn, :].rearrange("p (c i) t -> p c t i", i=4),
+                in_=src.rearrange("p t (c i) -> p c t i", i=4),
+            )
+
+        def gather_second(c0, cn):
+            g4 = ring2.tile([P, 4, cn], F32, name="g4")
+            for t in range(4):
+                look_up(g4[:, t, :], 1, t, c0, cn)
+            return g4
+
+        def quantize_g(s, c0, cn):
             nc.vector.quantize_mx(
-                out=codes[e][:, s, :].bitcast(E4M3X4), scales=scales_g[e][:, s, :], in_=grouped[e, s][:].rearrange("p n t -> p (n t)")
+                out=codes[:, s, c0 : c0 + cn].bitcast(E4M3X4),
+                scales=scales_g[:, s, c0 : c0 + cn],
+                in_=grouped[s][:, c0 : c0 + cn, :].rearrange("p n t -> p (n t)"),
             )
 
         dh = {}
 
         def first_product(e, h):
-            cols = slice(h * HALF, (h + 1) * HALF)
+            cols = slice(e * C + h * HALF, e * C + (h + 1) * HALF)
             dht = psum.tile([P, H], F32, name="dht")
             for s in range(NPASS):
                 nc.tensor.matmul_mx(
                     out=dht[:],
-                    lhsT=codes[e][:, s, cols].bitcast(E4M3X4),
-                    lhsT_scale=scales_g[e][:, s, cols],
+                    lhsT=codes[:, s, cols].bitcast(E4M3X4),
+                    lhsT_scale=scales_g[:, s, cols],
                     rhs=w2_t[:, e * NPASS + s, :].bitcast(E2M1X4),
                     rhs_scale=w2s_t[:, e * NPASS + s, :],
                     start=(s == 0),
                     stop=(s == NPASS - 1),
                 )
-            turned = ring3.tile([P, 4, P], F32, name="turned")
+            turned = ring2.tile([P, 4, P], F32, name="turned")
             nc.scalar.copy(out=turned[:], in_=dht[:].rearrange("p (q t) -> p t q", t=4))
             bank = psum.tile([P, 4, HALF], F32, name="bank")
             for t in range(4):
                 nc.tensor.transpose(bank[:, t, :], turned[:, t, :], ident[:])
             dh[e, h] = bank
 
-        silu_t = keep.tile([P, 4, S], F32, name="silu_t")
-        nsilu_t = keep.tile([P, 4, S], F32, name="nsilu_t")
-        sig_t = keep.tile([P, 4, S], F32, name="sig_t")
-        f1_t = keep.tile([P, 4, S], F32, name="f1_t")
+        silu_t = [keep.tile([P, 4, 2 * C], F32, name=f"silu_t{i}") for i in range(2)]
+        nsilu_t = keep.tile([P, S, 4], F32, name="nsilu_t")
+        sig_t = [keep.tile([P, 4, 2 * C], F32, name=f"sig_t{i}") for i in range(2)]
 
-        def silus(e):
-            cols = slice(e * C, (e + 1) * C)
-            nc.scalar.activation(nsilu_t[:, :, cols], a1_t[:, :, cols], ACT.Silu, scale=-1.0)
-            nc.scalar.activation(silu_t[:, :, cols], a1_t[:, :, cols], ACT.Silu)
+        def nsilu(i):
+            cols = slice(2 * i * C, 2 * (i + 1) * C)
+            nc.scalar.activation(nsilu_t[:, cols, :], a1_t[i][:].rearrange("p t n -> p n t"), ACT.Silu, scale=-1.0)
 
-        def sigmoids(cols):
-            nc.scalar.activation(sig_t[:, :, cols], a1_t[:, :, cols], ACT.Sigmoid)
+        def silu(i):
+            nc.scalar.activation(silu_t[i][:], a1_t[i][:], ACT.Silu)
+
+        def sigmoid(i):
+            nc.scalar.activation(sig_t[i][:], a1_t[i][:], ACT.Sigmoid)
+
+        weighed = {}
+
+        def weigh(e, eng):
+            cols = slice(e % 2 * C, (e % 2 + 1) * C)
+            w = keep.tile([P, C, 4], F32, name="w")
+            eng.tensor_tensor(
+                w[:], sig_t[e // 2][:, :, cols].rearrange("p t n -> p n t"), a3_t[e][:].rearrange("p t n -> p n t"), MULT
+            )
+            weighed[e] = w
 
         def factor(e):
             cols = slice(e * C, (e + 1) * C)
-            nd = ring2.tile([P, 4, C], F32, name="nd")
-            nc.vector.scalar_tensor_tensor(nd[:], nsilu_t[:, :, cols], 1.0, sig_t[:, :, cols], SUB, MULT)
-            nc.vector.scalar_tensor_tensor(f1_t[:, :, cols], nd[:], -1.0, a3_t[:, :, cols], MULT, MULT)
+            nc.vector.scalar_tensor_tensor(nsilu_t[:, cols, :], nsilu_t[:, cols, :], 1.0, weighed[e][:], SUB, MULT)
 
         qd = {}
 
         def products(e, h):
-            da = ring3.tile([P, 2, HALF, 4], BF16, name="da", align_bytes=64)
+            da = ring2.tile([P, 2, HALF, 4], BF16, name="da", align_bytes=64)
             cols = slice(e * C + h * HALF, e * C + (h + 1) * HALF)
-            for j, f in enumerate((f1_t, silu_t)):
-                nc.vector.tensor_tensor(
-                    da[:, j].rearrange("p (c i) t -> p c t i", i=4),
-                    dh[e, h][:].rearrange("p t (c i) -> p c t i", i=4),
-                    f[:, :, cols].rearrange("p t (c i) -> p c t i", i=4),
-                    MULT,
-                )
+            bank = dh[e, h][:].rearrange("p t (c i) -> p c t i", i=4)
+            nc.vector.scalar_tensor_tensor(
+                da[:, 0], nsilu_t[:, cols, :], -1.0, dh[e, h][:].rearrange("p t n -> p n t"), MULT, MULT
+            )
+            nc.vector.tensor_tensor(
+                da[:, 1].rearrange("p (c i) t -> p c t i", i=4), bank, silu_t[e // 2][:, :, e % 2 * C + h * HALF : e % 2 * C + (h + 1) * HALF].rearrange("p t (c i) -> p c t i", i=4), MULT
+            )
             qd[e, h] = da
 
         def second(e, h):
@@ -207,7 +230,8 @@ def tile_moe_bdx_glu_silu_kernel(
                             start=(j == 0),
                             stop=(j == 1),
                         )
-                nc.scalar.copy(out=dx_t[:, k0 : k0 + kn, e * C + h * HALF : e * C + (h + 1) * HALF], in_=acc[:])
+                slots = slice(e * C + h * HALF, e * C + (h + 1) * HALF)
+                nc.scalar.copy(out=dx_t[:, k0 : k0 + kn, slots], in_=acc[:])
 
         def combine(kt, c0, cn, eng):
             cols = slice(c0 // 16, (c0 + cn) // 16)
@@ -219,39 +243,53 @@ def tile_moe_bdx_glu_silu_kernel(
             eng.tensor_tensor(o[:], r1[:], r2[:], ADD)
             nc.sync.dma_start(out=out[kt * P : (kt + 1) * P, c0 : c0 + cn], in_=o[:])
 
-        gather(0, 0)
-        gather(1, 0)
-        quantize_g(0, 0)
-        gather(0, 1)
-        quantize_g(1, 0)
-        silus(0)
-        gather(1, 1)
-        quantize_g(0, 1)
+        for t in range(4):
+            for i, (c0, cn) in enumerate(CUTS):
+                look_up(g_first[i][:, t, :], 0, t, c0, cn)
+
+        def first_half(i):
+            c0, cn = CUTS[i]
+            interleave(0, g_first[i][:], c0, cn)
+
+        nsilu(0)
+        first_half(0)
+        silu(0)
+        first_half(1)
+        g4 = gather_second(*CUTS[0])
+        interleave(1, g4[:], *CUTS[0])
+        quantize_g(0, 0, 256)
+        nsilu(1)
+        silu(1)
+        sigmoid(0)
+        g4 = gather_second(*CUTS[1])
+        quantize_g(1, 0, 256)
         first_product(0, 0)
-        silus(1)
-        gather(2, 0)
-        quantize_g(1, 1)
+        interleave(1, g4[:], *CUTS[1])
         first_product(0, 1)
-        sigmoids(slice(0, 2 * C))
-        gather(2, 1)
-        quantize_g(2, 0)
-        gather(3, 0)
-        quantize_g(2, 1)
-        silus(2)
-        silus(3)
-        gather(3, 1)
-        quantize_g(3, 0)
-        sigmoids(slice(2 * C, 4 * C))
+        quantize_g(0, 256, 256)
+        first_half(2)
+        weigh(0, nc.vector)
+        factor(0)
+        g4 = gather_second(*CUTS[2])
+        quantize_g(1, 256, 256)
+        interleave(1, g4[:], *CUTS[2])
+        sigmoid(1)
+        quantize_g(0, 512, 512)
+        dx_t = keep.tile([P, KT, S], F32, name="dx_t")
         for e in range(E):
-            factor(e)
-            if e == 0:
-                quantize_g(3, 1)
+            if e > 0:
+                weigh(e, nc.gpsimd)
+                factor(e)
+            if e == 1:
+                quantize_g(1, 512, 512)
             products(e, 0)
             if e + 1 < E:
                 first_product(e + 1, 0)
+            if e + 1 == E:
+                second(e, 0)
             products(e, 1)
-            second(e, 0)
             if e + 1 < E:
+                second(e, 0)
                 first_product(e + 1, 1)
             second(e, 1)
         for kt in range(KT - 1):

@@ -166,12 +166,11 @@ def tile_moe_bdx_glu_silu_kernel(
             dh[e, h] = bank
 
         silu_t = [keep.tile([P, 4, 2 * C], F32, name=f"silu_t{i}") for i in range(2)]
-        nsilu_t = keep.tile([P, S, 4], F32, name="nsilu_t")
+        nsilu_t = [keep.tile([P, 4, 2 * C], F32, name=f"nsilu_t{i}") for i in range(2)]
         sig_t = [keep.tile([P, 4, 2 * C], F32, name=f"sig_t{i}") for i in range(2)]
 
         def nsilu(i):
-            cols = slice(2 * i * C, 2 * (i + 1) * C)
-            nc.scalar.activation(nsilu_t[:, cols, :], a1_t[i][:].rearrange("p t n -> p n t"), ACT.Silu, scale=-1.0)
+            nc.scalar.activation(nsilu_t[i][:], a1_t[i][:], ACT.Silu, scale=-1.0)
 
         def silu(i):
             nc.scalar.activation(silu_t[i][:], a1_t[i][:], ACT.Silu)
@@ -183,27 +182,25 @@ def tile_moe_bdx_glu_silu_kernel(
 
         def weigh(e, eng):
             cols = slice(e % 2 * C, (e % 2 + 1) * C)
-            w = keep.tile([P, C, 4], F32, name="w")
-            eng.tensor_tensor(
-                w[:], sig_t[e // 2][:, :, cols].rearrange("p t n -> p n t"), a3_t[e][:].rearrange("p t n -> p n t"), MULT
-            )
+            w = keep.tile([P, 4, C], F32, name="w")
+            eng.tensor_tensor(w[:], sig_t[e // 2][:, :, cols], a3_t[e][:], MULT)
             weighed[e] = w
 
         def factor(e):
-            cols = slice(e * C, (e + 1) * C)
-            nc.vector.scalar_tensor_tensor(nsilu_t[:, cols, :], nsilu_t[:, cols, :], 1.0, weighed[e][:], SUB, MULT)
+            f = nsilu_t[e // 2][:, :, e % 2 * C : (e % 2 + 1) * C]
+            nc.vector.scalar_tensor_tensor(f, f, 1.0, weighed[e][:], SUB, MULT)
 
         qd = {}
 
         def products(e, h):
             da = ring2.tile([P, 2, HALF, 4], BF16, name="da", align_bytes=64)
-            cols = slice(e * C + h * HALF, e * C + (h + 1) * HALF)
+            cols = slice(e % 2 * C + h * HALF, e % 2 * C + (h + 1) * HALF)
             bank = dh[e, h][:].rearrange("p t (c i) -> p c t i", i=4)
             nc.vector.scalar_tensor_tensor(
-                da[:, 0], nsilu_t[:, cols, :], -1.0, dh[e, h][:].rearrange("p t n -> p n t"), MULT, MULT
+                da[:, 0], nsilu_t[e // 2][:, :, cols].rearrange("p t n -> p n t"), -1.0, dh[e, h][:].rearrange("p t n -> p n t"), MULT, MULT
             )
             nc.vector.tensor_tensor(
-                da[:, 1].rearrange("p (c i) t -> p c t i", i=4), bank, silu_t[e // 2][:, :, e % 2 * C + h * HALF : e % 2 * C + (h + 1) * HALF].rearrange("p t (c i) -> p c t i", i=4), MULT
+                da[:, 1].rearrange("p (c i) t -> p c t i", i=4), bank, silu_t[e // 2][:, :, cols].rearrange("p t (c i) -> p c t i", i=4), MULT
             )
             qd[e, h] = da
 

from contextlib import ExitStack

import concourse.mybir as mybir
from concourse.masks import make_identity

K, T, E, C, H, N = 768, 512, 4, 256, 512, 1024
S = E * C

FLOPS = 2 * S * (N * H + 2 * H * K)
BYTES = 4 * (N * T + 2 * H * S + S + K * T) + E * (N * H // 2 + N * H // 32) + 2 * E * (H * K // 2 + H * K // 32) + 2 * (S + 2 * T) * 8

F32 = mybir.dt.float32
BF16 = mybir.dt.bfloat16
U32 = mybir.dt.uint32
I32 = mybir.dt.int32
U16 = mybir.dt.uint16
U8 = mybir.dt.uint8
E4M3X4 = mybir.dt.float8_e4m3fn_x4
E2M1X4 = mybir.dt.float4_e2m1fn_x4
ACT = mybir.ActivationFunctionType
MULT = mybir.AluOpType.mult
SUB = mybir.AluOpType.subtract
ADD = mybir.AluOpType.add

P = 128
HALF = 128
NPASS = N // 512
KT = K // P
CUTS = ((0, 256), (256, 384), (640, 384))


def tile_moe_bdx_glu_silu_kernel(
    tc, dyT, a1, a3, w2_words, w2_scales, w1_words, w1_scales, w3_words, w3_scales, gate, offs, pos1, pos2, out
):
    nc = tc.nc
    with ExitStack() as ctx:
        keep = ctx.enter_context(tc.tile_pool(name="keep", bufs=1))
        ring3 = ctx.enter_context(tc.tile_pool(name="ring3", bufs=3))
        ring2 = ctx.enter_context(tc.tile_pool(name="ring2", bufs=2))
        psum = ctx.enter_context(tc.psum_pool(name="psum", bufs=2))

        offs_t = keep.tile([P, S // 16], U16, name="offs_t")
        pos1_t = keep.tile([P, T // 16], U16, name="pos1_t")
        pos2_t = keep.tile([P, T // 16], U16, name="pos2_t")
        dy = [[keep.tile([P, T], F32, name=f"dy{s}{t}") for t in range(4)] for s in range(NPASS)]
        gate_t = keep.tile([P, S], F32, name="gate_t")
        a1_t = [keep.tile([P, 4, 2 * C], F32, name=f"a1_t{i}") for i in range(2)]
        a3_t = [keep.tile([P, 4, C], F32, name=f"a3_t{e}") for e in range(E)]
        w2_t = keep.tile([P, E * NPASS, 2 * H], U8, name="w2_t", align_bytes=64)
        w2s_t = keep.tile([P, E * NPASS, H], U8, name="w2s_t", align_bytes=64)
        w13_t = [keep.tile([P, E, 2 * K], U8, name=f"w13_t{j}", align_bytes=64) for j in range(2)]
        w13s_t = [keep.tile([P, E, K], U8, name=f"w13s_t{j}", align_bytes=64) for j in range(2)]
        ident = keep.tile([P, P], F32, name="ident")
        dummy = keep.tile([P, 1], F32, name="dummy")

        nc.gpsimd.memset(w2s_t[:].bitcast(I32), 0)
        nc.gpsimd.memset(w13s_t[0][:].bitcast(I32), 0)
        nc.gpsimd.memset(w13s_t[1][:].bitcast(I32), 0)
        make_identity(nc, ident[:])

        def load_dy(s, t):
            rows = dyT[512 * s : 512 * (s + 1), :].rearrange("(p t) n -> t p n", t=4)
            nc.sync.dma_start(out=dy[s][t][:], in_=rows[t])

        def load_w2(e):
            src = w2_words.bitcast(I32).rearrange("e s p n -> p (e s) n")
            es = slice(e * NPASS, (e + 1) * NPASS)
            nc.sync.dma_start(out=w2_t[:, es, :].bitcast(I32), in_=src[:, es, :])

        def load_scales(dst, src):
            view = src.bitcast(I32).rearrange("e s (q r) i -> r q (e s) i", r=4)
            for r in range(4):
                nc.sync.dma_start(out=dst[:].bitcast(I32)[r : P : 32, :, :], in_=view[r])

        def load_a(dst, src, e):
            cols = slice(e * C, (e + 1) * C)
            nc.sync.dma_start(out=dst[e][:], in_=src.rearrange("(p t) n -> p t n", t=4)[:, :, cols])

        def load_a1(i):
            cols = slice(2 * i * C, 2 * (i + 1) * C)
            nc.sync.dma_start(out=a1_t[i][:], in_=a1.rearrange("(p t) n -> p t n", t=4)[:, :, cols])

        def load_gate(e):
            nc.sync.dma_start(out=gate_t[:, e * C : (e + 1) * C], in_=gate[0:P, e * C : (e + 1) * C])

        nc.vector.memset(dummy[:], 0.0)
        nc.scalar.activation(dummy[:], dummy[:], ACT.Silu)

        nc.scalar.dma_start(out=gate_t[:, 0:C], in_=gate[0:P, 0:C])
        nc.sync.dma_start(offs_t[:], offs)
        load_dy(0, 0)
        for e in range(1, E):
            load_gate(e)
        load_dy(0, 1)
        load_a1(0)
        load_dy(0, 2)
        load_dy(0, 3)
        load_a1(1)
        for t in range(4):
            load_dy(1, t)
        load_w2(0)
        load_scales(w2s_t, w2_scales)
        load_w2(1)
        load_a(a3_t, a3, 0)
        load_w2(2)
        load_w2(3)
        load_a(a3_t, a3, 1)
        for j, (words, scales) in enumerate(((w1_words, w1_scales), (w3_words, w3_scales))):
            nc.sync.dma_start(out=w13_t[j][:].bitcast(I32), in_=words.bitcast(I32).rearrange("e s p n -> p (e s) n"))
            load_scales(w13s_t[j], scales)
        load_a(a3_t, a3, 2)
        load_a(a3_t, a3, 3)
        nc.sync.dma_start(pos1_t[:], pos1)
        nc.sync.dma_start(pos2_t[:], pos2)

        codes = keep.tile([P, NPASS, S], U32, name="codes", align_bytes=64)
        scales_g = keep.tile([P, NPASS, S], U8, name="scales_g", align_bytes=64)
        grouped = [keep.tile([P, S, 4], BF16, name=f"grouped{s}", align_bytes=64) for s in range(NPASS)]

        g_first = [keep.tile([P, 4, cn], F32, name=f"g_first{c0}") for c0, cn in CUTS]

        def look_up(dst, s, t, c0, cn):
            nc.vector.tensor_tensor(
                dst, dy[s][t][:].indirect(offs_t[:, c0 // 16 : (c0 + cn) // 16]), gate_t[:, c0 : c0 + cn], MULT
            )

        def interleave(s, src, c0, cn):
            nc.scalar.copy(
                out=grouped[s][:, c0 : c0 + cn, :].rearrange("p (c i) t -> p c t i", i=4),
                in_=src.rearrange("p t (c i) -> p c t i", i=4),
            )

        def gather_second(c0, cn):
            g4 = ring2.tile([P, 4, cn], F32, name="g4")
            for t in range(4):
                look_up(g4[:, t, :], 1, t, c0, cn)
            return g4

        def quantize_g(s, c0, cn):
            nc.vector.quantize_mx(
                out=codes[:, s, c0 : c0 + cn].bitcast(E4M3X4),
                scales=scales_g[:, s, c0 : c0 + cn],
                in_=grouped[s][:, c0 : c0 + cn, :].rearrange("p n t -> p (n t)"),
            )

        dh = {}

        def first_product(e, h):
            cols = slice(e * C + h * HALF, e * C + (h + 1) * HALF)
            dht = psum.tile([P, H], F32, name="dht")
            for s in range(NPASS):
                nc.tensor.matmul_mx(
                    out=dht[:],
                    lhsT=codes[:, s, cols].bitcast(E4M3X4),
                    lhsT_scale=scales_g[:, s, cols],
                    rhs=w2_t[:, e * NPASS + s, :].bitcast(E2M1X4),
                    rhs_scale=w2s_t[:, e * NPASS + s, :],
                    start=(s == 0),
                    stop=(s == NPASS - 1),
                )
            turned = ring2.tile([P, 4, P], F32, name="turned")
            nc.scalar.copy(out=turned[:], in_=dht[:].rearrange("p (q t) -> p t q", t=4))
            bank = psum.tile([P, 4, HALF], F32, name="bank")
            for t in range(4):
                nc.tensor.transpose(bank[:, t, :], turned[:, t, :], ident[:])
            dh[e, h] = bank

        silu_t = [keep.tile([P, 4, 2 * C], F32, name=f"silu_t{i}") for i in range(2)]
        nsilu_t = [keep.tile([P, 4, 2 * C], F32, name=f"nsilu_t{i}") for i in range(2)]
        sig_t = [keep.tile([P, 4, 2 * C], F32, name=f"sig_t{i}") for i in range(2)]

        def nsilu(i):
            nc.scalar.activation(nsilu_t[i][:], a1_t[i][:], ACT.Silu, scale=-1.0)

        def silu(i):
            nc.scalar.activation(silu_t[i][:], a1_t[i][:], ACT.Silu)

        def sigmoid(i):
            nc.scalar.activation(sig_t[i][:], a1_t[i][:], ACT.Sigmoid)

        weighed = {}

        def weigh(e, eng):
            cols = slice(e % 2 * C, (e % 2 + 1) * C)
            w = keep.tile([P, 4, C], F32, name="w")
            eng.tensor_tensor(w[:], sig_t[e // 2][:, :, cols], a3_t[e][:], MULT)
            weighed[e] = w

        def factor(e):
            f = nsilu_t[e // 2][:, :, e % 2 * C : (e % 2 + 1) * C]
            nc.vector.scalar_tensor_tensor(f, f, 1.0, weighed[e][:], SUB, MULT)

        qd = {}

        def products(e, h):
            da = ring2.tile([P, 2, HALF, 4], BF16, name="da", align_bytes=64)
            cols = slice(e % 2 * C + h * HALF, e % 2 * C + (h + 1) * HALF)
            bank = dh[e, h][:].rearrange("p t (c i) -> p c t i", i=4)
            nc.vector.scalar_tensor_tensor(
                da[:, 0], nsilu_t[e // 2][:, :, cols].rearrange("p t n -> p n t"), -1.0, dh[e, h][:].rearrange("p t n -> p n t"), MULT, MULT
            )
            nc.vector.tensor_tensor(
                da[:, 1].rearrange("p (c i) t -> p c t i", i=4), bank, silu_t[e // 2][:, :, cols].rearrange("p t (c i) -> p c t i", i=4), MULT
            )
            qd[e, h] = da

        def second(e, h):
            dc = ring3.tile([P, 2, HALF], U32, name="dc", align_bytes=64)
            ds = ring3.tile([P, 2, HALF], U8, name="ds", align_bytes=64)
            nc.vector.quantize_mx(
                out=dc[:].rearrange("p j n -> p (j n)").bitcast(E4M3X4),
                scales=ds[:].rearrange("p j n -> p (j n)"),
                in_=qd[e, h][:].rearrange("p j n t -> p (j n t)"),
            )
            groups = ((0, 1), (1, 2), (3, 3)) if (e, h) == (E - 1, 1) else ((0, 3), (3, 3))
            for i, (k0, kn) in enumerate(groups):
                acc = psum.tile([P, kn, HALF], F32, name=f"acc{i % 2}")
                for k in range(kn):
                    kt = k0 + k
                    for j in range(2):
                        nc.tensor.matmul_mx(
                            out=acc[:, k, :],
                            lhsT=w13_t[j][:, e, 2 * P * kt : 2 * P * (kt + 1)].bitcast(E2M1X4),
                            lhsT_scale=w13s_t[j][:, e, P * kt : P * (kt + 1)],
                            rhs=dc[:, j, :].bitcast(E4M3X4),
                            rhs_scale=ds[:, j, :],
                            start=(j == 0),
                            stop=(j == 1),
                        )
                slots = slice(e * C + h * HALF, e * C + (h + 1) * HALF)
                nc.scalar.copy(out=dx_t[:, k0 : k0 + kn, slots], in_=acc[:])

        def combine(kt, c0, cn, eng):
            cols = slice(c0 // 16, (c0 + cn) // 16)
            r1 = ring2.tile([P, cn], F32, name="r1")
            nc.vector.tensor_copy(r1[:], dx_t[:, kt, :].indirect(pos1_t[:, cols]))
            r2 = ring2.tile([P, cn], F32, name="r2")
            nc.vector.tensor_copy(r2[:], dx_t[:, kt, :].indirect(pos2_t[:, cols]))
            o = ring2.tile([P, cn], F32, name="o")
            eng.tensor_tensor(o[:], r1[:], r2[:], ADD)
            nc.sync.dma_start(out=out[kt * P : (kt + 1) * P, c0 : c0 + cn], in_=o[:])

        for t in range(4):
            for i, (c0, cn) in enumerate(CUTS):
                look_up(g_first[i][:, t, :], 0, t, c0, cn)

        def first_half(i):
            c0, cn = CUTS[i]
            interleave(0, g_first[i][:], c0, cn)

        nsilu(0)
        first_half(0)
        silu(0)
        first_half(1)
        g4 = gather_second(*CUTS[0])
        interleave(1, g4[:], *CUTS[0])
        quantize_g(0, 0, 256)
        nsilu(1)
        silu(1)
        sigmoid(0)
        g4 = gather_second(*CUTS[1])
        quantize_g(1, 0, 256)
        first_product(0, 0)
        interleave(1, g4[:], *CUTS[1])
        first_product(0, 1)
        quantize_g(0, 256, 256)
        first_half(2)
        weigh(0, nc.vector)
        factor(0)
        g4 = gather_second(*CUTS[2])
        quantize_g(1, 256, 256)
        interleave(1, g4[:], *CUTS[2])
        sigmoid(1)
        quantize_g(0, 512, 512)
        dx_t = keep.tile([P, KT, S], F32, name="dx_t")
        for e in range(E):
            if e > 0:
                weigh(e, nc.gpsimd)
                factor(e)
            if e == 1:
                quantize_g(1, 512, 512)
            products(e, 0)
            if e + 1 < E:
                first_product(e + 1, 0)
            if e + 1 == E:
                second(e, 0)
            products(e, 1)
            if e + 1 < E:
                second(e, 0)
                first_product(e + 1, 1)
            second(e, 1)
        for kt in range(KT - 1):
            combine(kt, 0, T, nc.gpsimd)
        combine(KT - 1, 0, T // 2, nc.vector)
        combine(KT - 1, T // 2, T // 2, nc.vector)
